import numpy as np
import ml_dtypes


def mxq(x, axis, fmt="e4m3"):
    dtype, down = {"e4m3": (ml_dtypes.float8_e4m3fn, 7), "e5m2": (ml_dtypes.float8_e5m2, 14)}[fmt]
    v = np.moveaxis(np.asarray(x, np.float32).astype(ml_dtypes.bfloat16).astype(np.float64), axis, -1)
    blocks = v.reshape(v.shape[:-1] + (-1, 32))
    amax = np.abs(blocks).max(-1, keepdims=True)
    byte = np.maximum(np.where(amax > 0, np.frexp(amax)[1] - 1 + 127, 0) - down, 1)
    scale = np.exp2(byte - 127.0)
    codes = (blocks / scale).astype(np.float32).astype(dtype).astype(np.float64)
    return np.moveaxis((codes * scale).reshape(v.shape), -1, axis)


WIDE = False


def mx_kscale(k):
    if not WIDE:
        return np.ones(k)
    levels = np.array([10, -10, 5, -5, 0])
    if k % 512:
        return np.exp2(np.random.permutation(np.resize(levels, k // 32))).repeat(32)
    a = np.empty((k // 512, 16))
    for p in range(k // 512):
        a[p, :8] = np.random.permutation(np.resize(levels, 8))
        for g in range(8):
            far = levels[np.abs(levels - a[p, g]) >= 10]
            a[p, g + 8] = far[np.random.randint(len(far))]
    return np.exp2(a.ravel()).repeat(32)


def f64(x):
    return np.asarray(x).astype(np.float64)


def striped(idx):
    return np.tile(idx.reshape(-1, 16).T, (8, 1)).astype(np.uint16)


def unstriped(offs):
    return offs[:16].T.reshape(-1).astype(np.int64)


def striped8(idx):
    return np.concatenate([x.reshape(-1, 16).T for x in idx]).astype(np.uint16)


def runs(offs, k):
    lists = np.stack([offs[16 * r : 16 * r + 16].T.reshape(-1) for r in range(8)]).astype(np.int64)
    return lists[np.arange(k) % 512 // 64]


def pack_weight(w):
    k, n = w.shape
    w = f64(np.asarray(w, np.float32).astype(ml_dtypes.bfloat16)).reshape(k // 32, 32, n)
    amax = np.abs(w).max(1)
    byte = np.clip(np.where(amax > 0, np.frexp(amax)[1] - 1 + 127 - 7, 1), 1, 254)
    scaled = (w * np.exp2(127.0 - byte)[:, None, :]).reshape(k, n).astype(np.float32)
    words = np.ascontiguousarray(scaled.reshape(k // 512, 128, 4, n).transpose(0, 1, 3, 2)).astype(ml_dtypes.float8_e4m3fn).view(np.uint8)
    return words, np.ascontiguousarray(byte.astype(np.uint8).reshape(k // 512, 16, n))


def unpack_weight(words, scales):
    g, p, n, _ = words.shape
    vals = np.ascontiguousarray(words).view(ml_dtypes.float8_e4m3fn).astype(np.float64) * np.repeat(np.exp2(scales.astype(np.float64) - 127.0), 8, axis=1)[..., None]
    return vals.transpose(0, 1, 3, 2).reshape(g * 512, n)


K, T, S, V, H, C = 512, 2048, 512, 256, 512, 512


def setup_inputs():
    n = np.random.standard_normal
    s = mx_kscale(K)[:, None]
    packed_xT = pack_weight(n((K, T)) * s)
    return {
        "x_words": packed_xT[0],
        "x_scales": packed_xT[1],
        "w1": (n((K, H)) / np.sqrt(K) / s).astype(np.float32),
        "gs": (np.random.uniform(0.5, 1.5, (K, 1)) / s).astype(np.float32),
        "wb": (n((K, V)) / np.sqrt(K) / s).astype(np.float32),
        "offs": striped(np.random.permutation(T)[:S]),
        "n1": striped8(np.stack([np.random.permutation(S) for _ in range(8)])),
        "cand": striped(np.random.permutation(T)[:C]),
        "cb": striped(np.random.permutation(T)[:C]),
        "n2": striped8(np.stack([np.random.permutation(V) for _ in range(8)])),
        "n3": striped8(np.stack([np.random.permutation(V) for _ in range(8)])),
    }


def reference(x_words, x_scales, w1, gs, wb, offs, n1, cand, cb, n2, n3):
    x_cand = unpack_weight(x_words, x_scales)[:, unstriped(cand)]
    xq = unpack_weight(x_words, x_scales)[:, unstriped(offs)]
    y = mxq(f64(w1), 0, "e4m3").T @ xq
    ln = y[np.arange(H)[:, None], runs(n1, H)]
    sq = (ln) ** 2
    ms = sq.reshape(H, V, 2).sum(axis=2)
    z = f64(gs) * np.sqrt(ms + 0.1)
    a = 0.0625 * ((x_cand.T @ mxq(z, 0, "e4m3")))
    x_cb = unpack_weight(x_words, x_scales)[:, unstriped(cb)]
    b = x_cb.T @ mxq(f64(wb), 0, "e4m3")
    return 0.75 * (a * (b[np.arange(C)[:, None], runs(n3, C)]) - ((a[np.arange(C)[:, None], runs(n2, C)]) * b))

@@ -1,0 +1,264 @@
+from contextlib import ExitStack
+
+import concourse.mybir as mybir
+
+F32 = mybir.dt.float32
+BF16 = mybir.dt.bfloat16
+I32 = mybir.dt.int32
+U32 = mybir.dt.uint32
+U16 = mybir.dt.uint16
+U8 = mybir.dt.uint8
+FP8X4 = mybir.dt.float8_e4m3fn_x4
+ALU = mybir.AluOpType
+ACT = mybir.ActivationFunctionType
+
+P = 128
+PACK = 4
+K, T, S, V, H, C = 512, 2048, 512, 256, 512, 512
+HALF_S = S // 2
+HALF_V = V // 2
+OUT_SCALE = 0.75 * 0.0625
+EPS = 0.1
+
+FLOPS = 2 * K * (H * S + 2 * C * V)
+
+
+def tile_picked_cdswcrossbhprms_none_p_kernel(
+    tc, x_words, x_scales, w1, gs, wb, offs, n1, cand, cb, n2, n3, out
+):
+    nc = tc.nc
+    with ExitStack() as ctx:
+        lists = ctx.enter_context(tc.tile_pool(name="lists", bufs=1))
+        sb = ctx.enter_context(tc.tile_pool(name="sb", bufs=1))
+        psum = ctx.enter_context(tc.psum_pool(name="psum", bufs=1))
+
+        def load_list(src, name):
+            tile = lists.tile(list(src.shape), U16, name=name)
+            nc.sync.dma_start(tile[:], src)
+            return tile
+
+        def new(shape, dtype, name, tag=None):
+            return sb.tile(shape, dtype, name=name, tag=tag or name, align_bytes=64)
+
+        table_scales = new([P, T], U8, "table_scales")
+        nc.vector.memset(table_scales[:].bitcast(I32), 0)
+        offs_sb = load_list(offs, "offs_sb")
+        for q in range(4):
+            nc.sync.dma_start(
+                table_scales[32 * q : 32 * q + 4, :].bitcast(I32),
+                x_scales[0, 4 * q : 4 * q + 4, :].bitcast(I32),
+            )
+        cb_sb = load_list(cb, "cb_sb")
+        w1_raw = new([P, PACK, H], F32, "w1_raw", tag="raw")
+        nc.sync.dma_start(w1_raw[:], w1.rearrange("(p j) c -> p j c", j=PACK))
+        table_words = new([P, T], I32, "table_words")
+        nc.sync.dma_start(table_words[:], x_words[0].rearrange("p n r -> p (n r)").bitcast(I32))
+        cand_sb = load_list(cand, "cand_sb")
+        n1_sb = load_list(n1, "n1_sb")
+        n3_sb = load_list(n3, "n3_sb")
+        n2_sb = load_list(n2, "n2_sb")
+        gs_sb = new([P, PACK], F32, "gs_sb")
+        nc.gpsimd.dma_start(gs_sb[:], gs.rearrange("(p t) o -> p (t o)", t=PACK))
+
+        def padded_window(name):
+            tile = new([P, 2 * V], F32, name)
+            nc.vector.memset(tile[:, V:], 0.0)
+            return tile
+
+        b_sb = [padded_window(f"b_sb{t}") for t in range(PACK)]
+        a_sb = [padded_window(f"a_sb{t}") for t in range(PACK)]
+
+        def gather_scales(list_sb, name, tag=None):
+            picked = new([P, S], U8, name, tag)
+            nc.vector.tensor_copy(picked[:], table_scales[:].indirect(list_sb[:]))
+            return picked
+
+        def deal_scales(picked, name):
+            dealt = new([P, C], U8, name)
+            nc.vector.tensor_copy(
+                dealt[:].rearrange("p (t m) -> p t m", t=PACK),
+                picked[:].rearrange("p (m t) -> p t m", t=PACK),
+            )
+            return dealt
+
+        xq_scales = gather_scales(offs_sb, "xq_scales")
+        cb_picked = gather_scales(cb_sb, "cb_picked")
+        cb_scales = deal_scales(cb_picked, "cb_scales")
+
+        w1_bf = []
+        for u in range(2):
+            pair = new([P, 2, P, PACK], BF16, f"w1_bf{u}")
+            cast = nc.scalar.copy if u == 0 else nc.vector.tensor_copy
+            cast(
+                pair[:].rearrange("p t m j -> p m j t"),
+                w1_raw[:].rearrange("p j (m t) -> p m j t", t=PACK)[:, :, :, 2 * u : 2 * u + 2],
+            )
+            w1_bf.append(pair)
+        wb_raw = new([P, PACK, V], F32, "wb_raw", tag="raw")
+        nc.sync.dma_start(wb_raw[:], wb.rearrange("(p j) v -> p j v", j=PACK))
+
+        def quantize_w1(u):
+            codes = new([P, 2 * P], U32, f"w1_codes{u}")
+            scales = new([P, 2 * P], U8, f"w1_scales{u}")
+            nc.vector.quantize_mx(
+                out=codes[:].bitcast(FP8X4),
+                scales=scales[:],
+                in_=w1_bf[u][:].rearrange("p t m j -> p (t m j)"),
+            )
+            return codes, scales
+
+        words = table_words[:].bitcast(U32)
+        w1_q = [quantize_w1(0), quantize_w1(1)]
+        xq_words = []
+        for h in range(2):
+            picked = new([P, HALF_S], U32, f"xq_words{h}")
+            nc.vector.tensor_copy(picked[:], words.indirect(offs_sb[:, 16 * h : 16 * (h + 1)]))
+            xq_words.append(picked)
+        y_ps = [psum.tile([P, S], F32, name=f"y_ps{t}", tag=f"bank{t}") for t in range(PACK)]
+        for u in range(2):
+            codes, scales = w1_q[u]
+            for h in range(2):
+                cols = slice(h * HALF_S, (h + 1) * HALF_S)
+                for e in range(2):
+                    rows = slice(e * P, (e + 1) * P)
+                    nc.tensor.matmul_mx(
+                        out=y_ps[2 * u + e][:, cols],
+                        lhsT=codes[:, rows].bitcast(FP8X4),
+                        lhsT_scale=scales[:, rows],
+                        rhs=xq_words[h][:].bitcast(FP8X4),
+                        rhs_scale=xq_scales[:, cols],
+                        start=True,
+                        stop=True,
+                    )
+
+        def gather_words_dealt(list_sb, name):
+            dealt = new([P, C], U32, name)
+            nc.vector.tensor_copy(
+                dealt[:].rearrange("p (t m) -> p m t", t=PACK), words.indirect(list_sb[:])
+            )
+            return dealt
+
+        cb_words = gather_words_dealt(cb_sb, "cb_words")
+        wb_bf = new([P, V, PACK], BF16, "wb_bf")
+        nc.vector.tensor_copy(
+            wb_bf[:].rearrange("p (c i) j -> p c j i", i=4),
+            wb_raw[:].rearrange("p j (c i) -> p c j i", i=4),
+        )
+        cand_picked = gather_scales(cand_sb, "cand_picked", tag="xq_scales")
+        wb_codes = new([P, V], U32, "wb_codes")
+        wb_scales = new([P, V], U8, "wb_scales")
+        nc.vector.quantize_mx(
+            out=wb_codes[:].bitcast(FP8X4),
+            scales=wb_scales[:],
+            in_=wb_bf[:].rearrange("p v j -> p (v j)"),
+        )
+        cand_words = gather_words_dealt(cand_sb, "cand_words")
+        cand_scales = deal_scales(cand_picked, "cand_scales")
+        lined = [new([P, PACK, HALF_S], F32, f"lined{h}") for h in range(2)]
+        ms = [new([P, PACK, HALF_V], F32, f"ms{h}") for h in range(2)]
+        a_lo = [psum.tile([P, 2, HALF_V], F32, name=f"a_lo{u}", tag=f"bank{u}") for u in range(2)]
+        a_hi = [psum.tile([P, HALF_V], F32, name=f"a_hi{t}", tag=f"bank{PACK + t}") for t in range(PACK)]
+        a_ps = [[a_lo[t // 2][:, t % 2, :] for t in range(PACK)], [a_hi[t][:] for t in range(PACK)]]
+        y_sq = []
+
+        def line_up(t, h):
+            nc.scalar.activation(
+                lined[h][:, t, :], y_sq[t][:].indirect(n1_sb[:, 16 * h : 16 * (h + 1)]), ACT.Copy
+            )
+
+        def add_pairs(h, t0, t1):
+            pairs = lined[h][:, t0:t1, :].rearrange("p t (v e) -> p (t v) e", e=2)
+            nc.vector.scalar_tensor_tensor(
+                ms[h][:, t0:t1, :].rearrange("p t v -> p (t v)"),
+                pairs[:, :, 0],
+                EPS,
+                pairs[:, :, 1],
+                ALU.add,
+                ALU.add,
+            )
+
+        def score(h):
+            root = new([P, PACK, HALF_V], F32, f"root{h}")
+            nc.scalar.activation(root[:], ms[h][:], ACT.Sqrt)
+            z_bf = new([P, HALF_V, PACK], BF16, f"z_bf{h}")
+            nc.vector.tensor_tensor(
+                z_bf[:].rearrange("p (c i) t -> p c t i", i=4),
+                root[:].rearrange("p t (c i) -> p c t i", i=4),
+                gs_sb[:].unsqueeze(1).unsqueeze(3).to_broadcast([P, HALF_V // 4, PACK, 4]),
+                ALU.mult,
+            )
+            z_codes = new([P, HALF_V], U32, f"z_codes{h}")
+            z_scales = new([P, HALF_V], U8, f"z_scales{h}")
+            nc.vector.quantize_mx(
+                out=z_codes[:].bitcast(FP8X4),
+                scales=z_scales[:],
+                in_=z_bf[:].rearrange("p v t -> p (v t)"),
+            )
+            for t in range(PACK):
+                rows = slice(t * P, (t + 1) * P)
+                nc.tensor.matmul_mx(
+                    out=a_ps[h][t],
+                    lhsT=cand_words[:, rows].bitcast(FP8X4),
+                    lhsT_scale=cand_scales[:, rows],
+                    rhs=z_codes[:].bitcast(FP8X4),
+                    rhs_scale=z_scales[:],
+                    start=True,
+                    stop=True,
+                )
+
+        def look_up_pairs(found, window, list_sb):
+            nc.scalar.activation(found, window[:].indirect(list_sb[:]), ACT.Copy)
+
+        for t in range(PACK):
+            sq = new([P, S], F32, f"y_sq{t}")
+            nc.scalar.activation(sq[:], y_ps[t][:], ACT.Square)
+            y_sq.append(sq)
+            line_up(t, 0)
+        add_pairs(0, 0, PACK)
+        b_banks = [psum.tile([P, 2, V], F32, name=f"b_bank{u}", tag=f"bank{2 + u}") for u in range(2)]
+        b_ps = [b_banks[t // 2][:, t % 2, :] for t in range(PACK)]
+        for t in range(PACK):
+            rows = slice(t * P, (t + 1) * P)
+            nc.tensor.matmul_mx(
+                out=b_ps[t],
+                lhsT=cb_words[:, rows].bitcast(FP8X4),
+                lhsT_scale=cb_scales[:, rows],
+                rhs=wb_codes[:].bitcast(FP8X4),
+                rhs_scale=wb_scales[:],
+                start=True,
+                stop=True,
+            )
+
+        for t in range(PACK):
+            nc.vector.tensor_copy(b_sb[t][:, :V], b_ps[t])
+        line_up(0, 1)
+        line_up(1, 1)
+        score(0)
+        line_up(2, 1)
+        add_pairs(1, 0, PACK - 1)
+        line_up(3, 1)
+        add_pairs(1, PACK - 1, PACK)
+        lo, hi = slice(0, HALF_V), slice(HALF_V, V)
+        for t in range(PACK):
+            nc.vector.tensor_scalar(a_sb[t][:, lo], a_ps[0][t], OUT_SCALE, None, ALU.mult)
+
+        b_n3_first = new([P, V], F32, "b_n3_first", tag=f"y_sq{PACK - 1}")
+        look_up_pairs(b_n3_first[:], b_sb[0], n3_sb)
+        b_n3_rest = new([P, PACK - 1, V], F32, "b_n3_rest", tag="ms1")
+        b_n3 = [b_n3_first[:]] + [b_n3_rest[:, t - 1, :] for t in range(1, PACK)]
+        score(1)
+        for t in range(1, PACK):
+            look_up_pairs(b_n3[t], b_sb[t], n3_sb)
+
+        out_rows = out.rearrange("(p t) v -> p t v", t=PACK)
+        for t in range(PACK):
+            nc.scalar.activation(a_sb[t][:, hi], a_ps[1][t], ACT.Copy, scale=OUT_SCALE)
+            first = new([P, V], F32, f"first{t}")
+            nc.vector.tensor_tensor(first[:], a_sb[t][:, :V], b_n3[t], ALU.mult)
+            a_n2 = new([P, V], F32, f"a_n2_{t}")
+            look_up_pairs(a_n2[:], a_sb[t], n2_sb)
+            second = new([P, V], F32, f"second{t}")
+            nc.vector.tensor_tensor(second[:], b_ps[t], a_n2[:], ALU.mult)
+            result = new([P, V], F32, f"result{t}")
+            nc.vector.tensor_tensor(result[:], first[:], second[:], ALU.subtract)
+            nc.sync.dma_start(out_rows[:, t, :], result[:])

@@ -43,22 +43,29 @@ def tile_picked_cdswcrossbhprms_none_p_kernel(
         table_scales = new([P, T], U8, "table_scales")
         nc.vector.memset(table_scales[:].bitcast(I32), 0)
         offs_sb = load_list(offs, "offs_sb")
+        cb_sb = load_list(cb, "cb_sb")
         for q in range(4):
             nc.sync.dma_start(
                 table_scales[32 * q : 32 * q + 4, :].bitcast(I32),
                 x_scales[0, 4 * q : 4 * q + 4, :].bitcast(I32),
             )
-        cb_sb = load_list(cb, "cb_sb")
-        w1_raw = new([P, PACK, H], F32, "w1_raw", tag="raw")
+        cand_sb = load_list(cand, "cand_sb")
+        w1_raw = new([P, PACK, H], F32, "w1_raw")
         nc.sync.dma_start(w1_raw[:], w1.rearrange("(p j) c -> p j c", j=PACK))
         table_words = new([P, T], I32, "table_words")
         nc.sync.dma_start(table_words[:], x_words[0].rearrange("p n r -> p (n r)").bitcast(I32))
-        cand_sb = load_list(cand, "cand_sb")
+        wb_raw = new([P, PACK, V], F32, "wb_raw")
+        nc.sync.dma_start(wb_raw[:], wb.rearrange("(p j) v -> p j v", j=PACK))
         n1_sb = load_list(n1, "n1_sb")
         n3_sb = load_list(n3, "n3_sb")
         n2_sb = load_list(n2, "n2_sb")
         gs_sb = new([P, PACK], F32, "gs_sb")
         nc.gpsimd.dma_start(gs_sb[:], gs.rearrange("(p t) o -> p (t o)", t=PACK))
+
+        warm_in = new([P, 1], F32, "warm_in")
+        nc.vector.memset(warm_in[:], 1.0)
+        warm_out = new([P, 1], F32, "warm_out")
+        nc.scalar.activation(warm_out[:], warm_in[:], ACT.Sqrt)
 
         def padded_window(name):
             tile = new([P, 2 * V], F32, name)
@@ -68,8 +75,8 @@ def tile_picked_cdswcrossbhprms_none_p_kernel(
         b_sb = [padded_window(f"b_sb{t}") for t in range(PACK)]
         a_sb = [padded_window(f"a_sb{t}") for t in range(PACK)]
 
-        def gather_scales(list_sb, name, tag=None):
-            picked = new([P, S], U8, name, tag)
+        def gather_scales(list_sb, name):
+            picked = new([P, S], U8, name)
             nc.vector.tensor_copy(picked[:], table_scales[:].indirect(list_sb[:]))
             return picked
 
@@ -83,37 +90,37 @@ def tile_picked_cdswcrossbhprms_none_p_kernel(
 
         xq_scales = gather_scales(offs_sb, "xq_scales")
         cb_picked = gather_scales(cb_sb, "cb_picked")
+        cand_picked = gather_scales(cand_sb, "cand_picked")
         cb_scales = deal_scales(cb_picked, "cb_scales")
+        cand_scales = deal_scales(cand_picked, "cand_scales")
 
-        w1_bf = []
-        for u in range(2):
-            pair = new([P, 2, P, PACK], BF16, f"w1_bf{u}")
-            cast = nc.scalar.copy if u == 0 else nc.vector.tensor_copy
-            cast(
+        def cast_w1(u):
+            pair = new([P, 2, P, PACK], BF16, f"w1_bf{u}", tag="w1_bf")
+            nc.scalar.copy(
                 pair[:].rearrange("p t m j -> p m j t"),
                 w1_raw[:].rearrange("p j (m t) -> p m j t", t=PACK)[:, :, :, 2 * u : 2 * u + 2],
             )
-            w1_bf.append(pair)
-        wb_raw = new([P, PACK, V], F32, "wb_raw", tag="raw")
-        nc.sync.dma_start(wb_raw[:], wb.rearrange("(p j) v -> p j v", j=PACK))
+            return pair
 
-        def quantize_w1(u):
+        def quantize_w1(pair, u):
             codes = new([P, 2 * P], U32, f"w1_codes{u}")
             scales = new([P, 2 * P], U8, f"w1_scales{u}")
             nc.vector.quantize_mx(
                 out=codes[:].bitcast(FP8X4),
                 scales=scales[:],
-                in_=w1_bf[u][:].rearrange("p t m j -> p (t m j)"),
+                in_=pair[:].rearrange("p t m j -> p (t m j)"),
             )
             return codes, scales
 
         words = table_words[:].bitcast(U32)
-        w1_q = [quantize_w1(0), quantize_w1(1)]
+        w1_q = [quantize_w1(cast_w1(0), 0)]
+        second_pair = cast_w1(1)
         xq_words = []
         for h in range(2):
             picked = new([P, HALF_S], U32, f"xq_words{h}")
             nc.vector.tensor_copy(picked[:], words.indirect(offs_sb[:, 16 * h : 16 * (h + 1)]))
             xq_words.append(picked)
+        w1_q.append(quantize_w1(second_pair, 1))
         y_ps = [psum.tile([P, S], F32, name=f"y_ps{t}", tag=f"bank{t}") for t in range(PACK)]
         for u in range(2):
             codes, scales = w1_q[u]
@@ -131,12 +138,15 @@ def tile_picked_cdswcrossbhprms_none_p_kernel(
                         stop=True,
                     )
 
-        def gather_words_dealt(list_sb, name):
-            dealt = new([P, C], U32, name)
+        def gather_words_dealt(list_sb, name, tag=None):
+            dealt = new([P, C], U32, name, tag)
             nc.vector.tensor_copy(
                 dealt[:].rearrange("p (t m) -> p m t", t=PACK), words.indirect(list_sb[:])
             )
             return dealt
+
+        y_last = new([P, S], F32, "y_last")
+        y_sq = [new([P, S], F32, f"y_sq{t}") for t in range(PACK)]
 
         cb_words = gather_words_dealt(cb_sb, "cb_words")
         wb_bf = new([P, V, PACK], BF16, "wb_bf")
@@ -144,7 +154,7 @@ def tile_picked_cdswcrossbhprms_none_p_kernel(
             wb_bf[:].rearrange("p (c i) j -> p c j i", i=4),
             wb_raw[:].rearrange("p j (c i) -> p c j i", i=4),
         )
-        cand_picked = gather_scales(cand_sb, "cand_picked", tag="xq_scales")
+        nc.vector.tensor_copy(y_last[:], y_ps[PACK - 1][:])
         wb_codes = new([P, V], U32, "wb_codes")
         wb_scales = new([P, V], U8, "wb_scales")
         nc.vector.quantize_mx(
@@ -152,22 +162,22 @@ def tile_picked_cdswcrossbhprms_none_p_kernel(
             scales=wb_scales[:],
             in_=wb_bf[:].rearrange("p v j -> p (v j)"),
         )
-        cand_words = gather_words_dealt(cand_sb, "cand_words")
-        cand_scales = deal_scales(cand_picked, "cand_scales")
-        lined = [new([P, PACK, HALF_S], F32, f"lined{h}") for h in range(2)]
+        nc.vector.tensor_tensor(y_sq[PACK - 1][:], y_last[:], y_last[:], ALU.mult)
+        cand_words = gather_words_dealt(cand_sb, "cand_words", tag="wb_bf")
+
+        lined_lo = new([P, PACK, HALF_S], F32, "lined_lo")
         ms = [new([P, PACK, HALF_V], F32, f"ms{h}") for h in range(2)]
         a_lo = [psum.tile([P, 2, HALF_V], F32, name=f"a_lo{u}", tag=f"bank{u}") for u in range(2)]
         a_hi = [psum.tile([P, HALF_V], F32, name=f"a_hi{t}", tag=f"bank{PACK + t}") for t in range(PACK)]
         a_ps = [[a_lo[t // 2][:, t % 2, :] for t in range(PACK)], [a_hi[t][:] for t in range(PACK)]]
-        y_sq = []
 
-        def line_up(t, h):
+        def line_up(lined, t, h):
             nc.scalar.activation(
-                lined[h][:, t, :], y_sq[t][:].indirect(n1_sb[:, 16 * h : 16 * (h + 1)]), ACT.Copy
+                lined, y_sq[t][:].indirect(n1_sb[:, 16 * h : 16 * (h + 1)]), ACT.Copy
             )
 
-        def add_pairs(h, t0, t1):
-            pairs = lined[h][:, t0:t1, :].rearrange("p t (v e) -> p (t v) e", e=2)
+        def add_pairs(lined, h, t0, t1):
+            pairs = lined.rearrange("p t (v e) -> p (t v) e", e=2)
             nc.vector.scalar_tensor_tensor(
                 ms[h][:, t0:t1, :].rearrange("p t v -> p (t v)"),
                 pairs[:, :, 0],
@@ -210,11 +220,10 @@ def tile_picked_cdswcrossbhprms_none_p_kernel(
             nc.scalar.activation(found, window[:].indirect(list_sb[:]), ACT.Copy)
 
         for t in range(PACK):
-            sq = new([P, S], F32, f"y_sq{t}")
-            nc.scalar.activation(sq[:], y_ps[t][:], ACT.Square)
-            y_sq.append(sq)
-            line_up(t, 0)
-        add_pairs(0, 0, PACK)
+            if t < PACK - 1:
+                nc.scalar.activation(y_sq[t][:], y_ps[t][:], ACT.Square)
+            line_up(lined_lo[:, t, :], t, 0)
+        add_pairs(lined_lo[:], 0, 0, PACK)
         b_banks = [psum.tile([P, 2, V], F32, name=f"b_bank{u}", tag=f"bank{2 + u}") for u in range(2)]
         b_ps = [b_banks[t // 2][:, t % 2, :] for t in range(PACK)]
         for t in range(PACK):
@@ -231,34 +240,32 @@ def tile_picked_cdswcrossbhprms_none_p_kernel(
 
         for t in range(PACK):
             nc.vector.tensor_copy(b_sb[t][:, :V], b_ps[t])
-        line_up(0, 1)
-        line_up(1, 1)
+        lined_hi = new([P, PACK, HALF_S], F32, "lined_hi")
+        for t in range(PACK):
+            line_up(lined_hi[:, t, :], t, 1)
+            if t % 2 == 1:
+                add_pairs(lined_hi[:, t - 1 : t + 1, :], 1, t - 1, t + 1)
         score(0)
-        line_up(2, 1)
-        add_pairs(1, 0, PACK - 1)
-        line_up(3, 1)
-        add_pairs(1, PACK - 1, PACK)
+        score(1)
         lo, hi = slice(0, HALF_V), slice(HALF_V, V)
         for t in range(PACK):
             nc.vector.tensor_scalar(a_sb[t][:, lo], a_ps[0][t], OUT_SCALE, None, ALU.mult)
-
-        b_n3_first = new([P, V], F32, "b_n3_first", tag=f"y_sq{PACK - 1}")
-        look_up_pairs(b_n3_first[:], b_sb[0], n3_sb)
-        b_n3_rest = new([P, PACK - 1, V], F32, "b_n3_rest", tag="ms1")
-        b_n3 = [b_n3_first[:]] + [b_n3_rest[:, t - 1, :] for t in range(1, PACK)]
-        score(1)
-        for t in range(1, PACK):
+        b_n3_all = new([P, PACK, V], F32, "b_n3_all", tag="lined_hi")
+        b_n3 = [b_n3_all[:, t, :] for t in range(PACK)]
+        for t in range(PACK):
             look_up_pairs(b_n3[t], b_sb[t], n3_sb)
 
+        for t in range(PACK):
+            nc.vector.tensor_scalar(a_sb[t][:, hi], a_ps[1][t], OUT_SCALE, None, ALU.mult)
+        first = [new([P, V], F32, f"first{t}") for t in range(PACK)]
+        for t in range(PACK):
+            nc.vector.tensor_tensor(first[t][:], a_sb[t][:, :V], b_n3[t], ALU.mult)
         out_rows = out.rearrange("(p t) v -> p t v", t=PACK)
         for t in range(PACK):
-            nc.scalar.activation(a_sb[t][:, hi], a_ps[1][t], ACT.Copy, scale=OUT_SCALE)
-            first = new([P, V], F32, f"first{t}")
-            nc.vector.tensor_tensor(first[:], a_sb[t][:, :V], b_n3[t], ALU.mult)
             a_n2 = new([P, V], F32, f"a_n2_{t}")
             look_up_pairs(a_n2[:], a_sb[t], n2_sb)
             second = new([P, V], F32, f"second{t}")
             nc.vector.tensor_tensor(second[:], b_ps[t], a_n2[:], ALU.mult)
             result = new([P, V], F32, f"result{t}")
-            nc.vector.tensor_tensor(result[:], first[:], second[:], ALU.subtract)
+            nc.vector.tensor_tensor(result[:], first[t][:], second[:], ALU.subtract)
             nc.sync.dma_start(out_rows[:, t, :], result[:])

@@ -67,21 +67,23 @@ def tile_picked_cdswcrossbhprms_none_p_kernel(
         warm_out = new([P, 1], F32, "warm_out")
         nc.scalar.activation(warm_out[:], warm_in[:], ACT.Sqrt)
 
-        def padded_window(name):
-            tile = new([P, 2 * V], F32, name)
-            nc.vector.memset(tile[:, V:], 0.0)
+        def padded_window(engine, width, name):
+            tile = new([P, 2 * width], F32, name)
+            engine.memset(tile[:, width:], 0.0)
             return tile
 
-        b_sb = [padded_window(f"b_sb{t}") for t in range(PACK)]
-        a_sb = [padded_window(f"a_sb{t}") for t in range(PACK)]
+        y_sq = [padded_window(nc.vector, S, f"y_sq{t}") for t in range(PACK - 1)]
+        y_sq.append(new([P, S], F32, f"y_sq{PACK - 1}"))
+        b_sb = [padded_window(nc.gpsimd, V, f"b_sb{t}") for t in range(PACK)]
+        a_sb = [padded_window(nc.gpsimd, V, f"a_sb{t}") for t in range(PACK)]
 
         def gather_scales(list_sb, name):
             picked = new([P, S], U8, name)
             nc.vector.tensor_copy(picked[:], table_scales[:].indirect(list_sb[:]))
             return picked
 
-        def deal_scales(picked, name):
-            dealt = new([P, C], U8, name)
+        def deal_scales(picked, name, tag=None):
+            dealt = new([P, C], U8, name, tag)
             nc.vector.tensor_copy(
                 dealt[:].rearrange("p (t m) -> p t m", t=PACK),
                 picked[:].rearrange("p (m t) -> p t m", t=PACK),
@@ -92,10 +94,9 @@ def tile_picked_cdswcrossbhprms_none_p_kernel(
         cb_picked = gather_scales(cb_sb, "cb_picked")
         cand_picked = gather_scales(cand_sb, "cand_picked")
         cb_scales = deal_scales(cb_picked, "cb_scales")
-        cand_scales = deal_scales(cand_picked, "cand_scales")
 
         def cast_w1(u):
-            pair = new([P, 2, P, PACK], BF16, f"w1_bf{u}", tag="w1_bf")
+            pair = new([P, 2, P, PACK], BF16, f"w1_bf{u}")
             nc.scalar.copy(
                 pair[:].rearrange("p t m j -> p m j t"),
                 w1_raw[:].rearrange("p j (m t) -> p m j t", t=PACK)[:, :, :, 2 * u : 2 * u + 2],
@@ -103,8 +104,8 @@ def tile_picked_cdswcrossbhprms_none_p_kernel(
             return pair
 
         def quantize_w1(pair, u):
-            codes = new([P, 2 * P], U32, f"w1_codes{u}")
-            scales = new([P, 2 * P], U8, f"w1_scales{u}")
+            codes = new([P, 2 * P], U32, f"w1_codes{u}", tag="w1_codes")
+            scales = new([P, 2 * P], U8, f"w1_scales{u}", tag="w1_scales")
             nc.vector.quantize_mx(
                 out=codes[:].bitcast(FP8X4),
                 scales=scales[:],
@@ -113,30 +114,36 @@ def tile_picked_cdswcrossbhprms_none_p_kernel(
             return codes, scales
 
         words = table_words[:].bitcast(U32)
-        w1_q = [quantize_w1(cast_w1(0), 0)]
-        second_pair = cast_w1(1)
+        w1_bf = [cast_w1(u) for u in range(2)]
+        codes, scales = quantize_w1(w1_bf[0], 0)
         xq_words = []
         for h in range(2):
             picked = new([P, HALF_S], U32, f"xq_words{h}")
             nc.vector.tensor_copy(picked[:], words.indirect(offs_sb[:, 16 * h : 16 * (h + 1)]))
             xq_words.append(picked)
-        w1_q.append(quantize_w1(second_pair, 1))
-        y_ps = [psum.tile([P, S], F32, name=f"y_ps{t}", tag=f"bank{t}") for t in range(PACK)]
-        for u in range(2):
-            codes, scales = w1_q[u]
+
+        def project(dest, codes, scales, e, h):
+            rows = slice(e * P, (e + 1) * P)
+            nc.tensor.matmul_mx(
+                out=dest,
+                lhsT=codes[:, rows].bitcast(FP8X4),
+                lhsT_scale=scales[:, rows],
+                rhs=xq_words[h][:].bitcast(FP8X4),
+                rhs_scale=xq_scales[:, h * HALF_S : (h + 1) * HALF_S],
+                start=True,
+                stop=True,
+            )
+
+        for h in range(2):
+            for t in range(2):
+                half = psum.tile([P, HALF_S], F32, name=f"y_half{t}{h}", tag=f"bank{4 * (1 - h) + t}")
+                project(half[:], codes, scales, t, h)
+                nc.scalar.activation(y_sq[t][:, h * HALF_S : (h + 1) * HALF_S], half[:], ACT.Square)
+        codes, scales = quantize_w1(w1_bf[1], 1)
+        y_ps = {t: psum.tile([P, S], F32, name=f"y_ps{t}", tag=f"bank{t}") for t in (2, 3)}
+        for t in (2, 3):
             for h in range(2):
-                cols = slice(h * HALF_S, (h + 1) * HALF_S)
-                for e in range(2):
-                    rows = slice(e * P, (e + 1) * P)
-                    nc.tensor.matmul_mx(
-                        out=y_ps[2 * u + e][:, cols],
-                        lhsT=codes[:, rows].bitcast(FP8X4),
-                        lhsT_scale=scales[:, rows],
-                        rhs=xq_words[h][:].bitcast(FP8X4),
-                        rhs_scale=xq_scales[:, cols],
-                        start=True,
-                        stop=True,
-                    )
+                project(y_ps[t][:, h * HALF_S : (h + 1) * HALF_S], codes, scales, t - 2, h)
 
         def gather_words_dealt(list_sb, name, tag=None):
             dealt = new([P, C], U32, name, tag)
@@ -146,7 +153,6 @@ def tile_picked_cdswcrossbhprms_none_p_kernel(
             return dealt
 
         y_last = new([P, S], F32, "y_last")
-        y_sq = [new([P, S], F32, f"y_sq{t}") for t in range(PACK)]
 
         cb_words = gather_words_dealt(cb_sb, "cb_words")
         wb_bf = new([P, V, PACK], BF16, "wb_bf")
@@ -154,7 +160,7 @@ def tile_picked_cdswcrossbhprms_none_p_kernel(
             wb_bf[:].rearrange("p (c i) j -> p c j i", i=4),
             wb_raw[:].rearrange("p j (c i) -> p c j i", i=4),
         )
-        nc.vector.tensor_copy(y_last[:], y_ps[PACK - 1][:])
+        cand_words = gather_words_dealt(cand_sb, "cand_words", tag="w1_bf1")
         wb_codes = new([P, V], U32, "wb_codes")
         wb_scales = new([P, V], U8, "wb_scales")
         nc.vector.quantize_mx(
@@ -162,47 +168,77 @@ def tile_picked_cdswcrossbhprms_none_p_kernel(
             scales=wb_scales[:],
             in_=wb_bf[:].rearrange("p v j -> p (v j)"),
         )
+        nc.vector.tensor_copy(y_last[:], y_ps[PACK - 1][:])
         nc.vector.tensor_tensor(y_sq[PACK - 1][:], y_last[:], y_last[:], ALU.mult)
-        cand_words = gather_words_dealt(cand_sb, "cand_words", tag="wb_bf")
 
-        lined_lo = new([P, PACK, HALF_S], F32, "lined_lo")
-        ms = [new([P, PACK, HALF_V], F32, f"ms{h}") for h in range(2)]
-        a_lo = [psum.tile([P, 2, HALF_V], F32, name=f"a_lo{u}", tag=f"bank{u}") for u in range(2)]
-        a_hi = [psum.tile([P, HALF_V], F32, name=f"a_hi{t}", tag=f"bank{PACK + t}") for t in range(PACK)]
-        a_ps = [[a_lo[t // 2][:, t % 2, :] for t in range(PACK)], [a_hi[t][:] for t in range(PACK)]]
+        b_banks = [psum.tile([P, 2, V], F32, name=f"b_bank{u}", tag=f"bank{6 + u}") for u in range(2)]
+        b_ps = [b_banks[t // 2][:, t % 2, :] for t in range(PACK)]
+        for t in range(PACK):
+            rows = slice(t * P, (t + 1) * P)
+            nc.tensor.matmul_mx(
+                out=b_ps[t],
+                lhsT=cb_words[:, rows].bitcast(FP8X4),
+                lhsT_scale=cb_scales[:, rows],
+                rhs=wb_codes[:].bitcast(FP8X4),
+                rhs_scale=wb_scales[:],
+                start=True,
+                stop=True,
+            )
 
-        def line_up(lined, t, h):
+        cand_scales = deal_scales(cand_picked, "cand_scales", tag="xq_scales")
+
+        lined = new([P, PACK, S], F32, "lined")
+        ms = new([P, PACK, V], F32, "ms")
+        halves = (slice(0, HALF_V), slice(HALF_V, V))
+
+        def add_pairs(dest, entries):
+            pairs = entries.rearrange("p (v e) -> p v e", e=2)
+            nc.vector.scalar_tensor_tensor(dest, pairs[:, :, 0], EPS, pairs[:, :, 1], ALU.add, ALU.add)
+
+        nc.scalar.activation(y_sq[2][:, :S], y_ps[2][:], ACT.Square)
+        last = PACK - 1
+        for t in range(last):
+            nc.scalar.activation(lined[:, t, :], y_sq[t][:].indirect(n1_sb[:]), ACT.Copy)
+        for h in range(2):
             nc.scalar.activation(
-                lined, y_sq[t][:].indirect(n1_sb[:, 16 * h : 16 * (h + 1)]), ACT.Copy
+                lined[:, last, h * HALF_S : (h + 1) * HALF_S],
+                y_sq[last][:].indirect(n1_sb[:, 16 * h : 16 * (h + 1)]),
+                ACT.Copy,
             )
+        for t in range(2):
+            nc.vector.tensor_copy(b_sb[t][:, :V], b_ps[t])
+        add_pairs(
+            ms[:, :last, :].rearrange("p t v -> p (t v)"),
+            lined[:, :last, :].rearrange("p t s -> p (t s)"),
+        )
+        for h in range(2):
+            add_pairs(ms[:, last, halves[h]], lined[:, last, h * HALF_S : (h + 1) * HALF_S])
+        for t in range(2, PACK):
+            nc.vector.tensor_copy(b_sb[t][:, :V], b_ps[t])
 
-        def add_pairs(lined, h, t0, t1):
-            pairs = lined.rearrange("p t (v e) -> p (t v) e", e=2)
-            nc.vector.scalar_tensor_tensor(
-                ms[h][:, t0:t1, :].rearrange("p t v -> p (t v)"),
-                pairs[:, :, 0],
-                EPS,
-                pairs[:, :, 1],
-                ALU.add,
-                ALU.add,
-            )
-
-        def score(h):
+        z_bf = []
+        for h in range(2):
             root = new([P, PACK, HALF_V], F32, f"root{h}")
-            nc.scalar.activation(root[:], ms[h][:], ACT.Sqrt)
-            z_bf = new([P, HALF_V, PACK], BF16, f"z_bf{h}")
+            nc.scalar.activation(root[:], ms[:, :, halves[h]], ACT.Sqrt)
+            half = new([P, HALF_V, PACK], BF16, f"z_bf{h}")
             nc.vector.tensor_tensor(
-                z_bf[:].rearrange("p (c i) t -> p c t i", i=4),
+                half[:].rearrange("p (c i) t -> p c t i", i=4),
                 root[:].rearrange("p t (c i) -> p c t i", i=4),
                 gs_sb[:].unsqueeze(1).unsqueeze(3).to_broadcast([P, HALF_V // 4, PACK, 4]),
                 ALU.mult,
             )
+            z_bf.append(half)
+
+        a_lo = [psum.tile([P, 2, HALF_V], F32, name=f"a_lo{u}", tag=f"bank{u}") for u in range(2)]
+        a_hi = [psum.tile([P, HALF_V], F32, name=f"a_hi{t}", tag=f"bank{2 + t}") for t in range(PACK)]
+        a_ps = [[a_lo[t // 2][:, t % 2, :] for t in range(PACK)], [a_hi[t][:] for t in range(PACK)]]
+        for h in range(2):
             z_codes = new([P, HALF_V], U32, f"z_codes{h}")
             z_scales = new([P, HALF_V], U8, f"z_scales{h}")
             nc.vector.quantize_mx(
                 out=z_codes[:].bitcast(FP8X4),
                 scales=z_scales[:],
-                in_=z_bf[:].rearrange("p v t -> p (v t)"),
+                in_=z_bf[h][:].rearrange("p v t -> p (v t)"),
             )
             for t in range(PACK):
                 rows = slice(t * P, (t + 1) * P)
@@ -219,47 +255,28 @@ def tile_picked_cdswcrossbhprms_none_p_kernel(
         def look_up_pairs(found, window, list_sb):
             nc.scalar.activation(found, window[:].indirect(list_sb[:]), ACT.Copy)
 
-        for t in range(PACK):
-            if t < PACK - 1:
-                nc.scalar.activation(y_sq[t][:], y_ps[t][:], ACT.Square)
-            line_up(lined_lo[:, t, :], t, 0)
-        add_pairs(lined_lo[:], 0, 0, PACK)
-        b_banks = [psum.tile([P, 2, V], F32, name=f"b_bank{u}", tag=f"bank{2 + u}") for u in range(2)]
-        b_ps = [b_banks[t // 2][:, t % 2, :] for t in range(PACK)]
-        for t in range(PACK):
-            rows = slice(t * P, (t + 1) * P)
-            nc.tensor.matmul_mx(
-                out=b_ps[t],
-                lhsT=cb_words[:, rows].bitcast(FP8X4),
-                lhsT_scale=cb_scales[:, rows],
-                rhs=wb_codes[:].bitcast(FP8X4),
-                rhs_scale=wb_scales[:],
-                start=True,
-                stop=True,
-            )
-
-        for t in range(PACK):
-            nc.vector.tensor_copy(b_sb[t][:, :V], b_ps[t])
-        lined_hi = new([P, PACK, HALF_S], F32, "lined_hi")
-        for t in range(PACK):
-            line_up(lined_hi[:, t, :], t, 1)
-            if t % 2 == 1:
-                add_pairs(lined_hi[:, t - 1 : t + 1, :], 1, t - 1, t + 1)
-        score(0)
-        score(1)
-        lo, hi = slice(0, HALF_V), slice(HALF_V, V)
-        for t in range(PACK):
-            nc.vector.tensor_scalar(a_sb[t][:, lo], a_ps[0][t], OUT_SCALE, None, ALU.mult)
-        b_n3_all = new([P, PACK, V], F32, "b_n3_all", tag="lined_hi")
+        b_n3_all = new([P, PACK, V], F32, "b_n3_all", tag="lined")
         b_n3 = [b_n3_all[:, t, :] for t in range(PACK)]
         for t in range(PACK):
             look_up_pairs(b_n3[t], b_sb[t], n3_sb)
 
         for t in range(PACK):
-            nc.vector.tensor_scalar(a_sb[t][:, hi], a_ps[1][t], OUT_SCALE, None, ALU.mult)
+            for h in range(2):
+                nc.vector.tensor_scalar(a_sb[t][:, halves[h]], a_ps[h][t], OUT_SCALE, None, ALU.mult)
         first = [new([P, V], F32, f"first{t}") for t in range(PACK)]
         for t in range(PACK):
-            nc.vector.tensor_tensor(first[t][:], a_sb[t][:, :V], b_n3[t], ALU.mult)
+            if t < 2:
+                for h in range(2):
+                    nc.vector.scalar_tensor_tensor(
+                        first[t][:, halves[h]],
+                        a_ps[h][t],
+                        OUT_SCALE,
+                        b_n3[t][:, halves[h]],
+                        ALU.mult,
+                        ALU.mult,
+                    )
+            else:
+                nc.gpsimd.tensor_tensor(first[t][:], a_sb[t][:, :V], b_n3[t], ALU.mult)
         out_rows = out.rearrange("(p t) v -> p t v", t=PACK)
         for t in range(PACK):
             a_n2 = new([P, V], F32, f"a_n2_{t}")

from contextlib import ExitStack

import concourse.mybir as mybir

F32 = mybir.dt.float32
BF16 = mybir.dt.bfloat16
I32 = mybir.dt.int32
U32 = mybir.dt.uint32
U16 = mybir.dt.uint16
U8 = mybir.dt.uint8
FP8X4 = mybir.dt.float8_e4m3fn_x4
ALU = mybir.AluOpType
ACT = mybir.ActivationFunctionType

P = 128
PACK = 4
K, T, S, V, H, C = 512, 2048, 512, 256, 512, 512
HALF_S = S // 2
HALF_V = V // 2
OUT_SCALE = 0.75 * 0.0625
EPS = 0.1

FLOPS = 2 * K * (H * S + 2 * C * V)


def tile_picked_cdswcrossbhprms_none_p_kernel(
    tc, x_words, x_scales, w1, gs, wb, offs, n1, cand, cb, n2, n3, out
):
    nc = tc.nc
    with ExitStack() as ctx:
        lists = ctx.enter_context(tc.tile_pool(name="lists", bufs=1))
        sb = ctx.enter_context(tc.tile_pool(name="sb", bufs=1))
        psum = ctx.enter_context(tc.psum_pool(name="psum", bufs=1))

        def load_list(src, name):
            tile = lists.tile(list(src.shape), U16, name=name)
            nc.sync.dma_start(tile[:], src)
            return tile

        def new(shape, dtype, name, tag=None):
            return sb.tile(shape, dtype, name=name, tag=tag or name, align_bytes=64)

        table_scales = new([P, T], U8, "table_scales")
        nc.vector.memset(table_scales[:].bitcast(I32), 0)
        offs_sb = load_list(offs, "offs_sb")
        cb_sb = load_list(cb, "cb_sb")
        for q in range(4):
            nc.sync.dma_start(
                table_scales[32 * q : 32 * q + 4, :].bitcast(I32),
                x_scales[0, 4 * q : 4 * q + 4, :].bitcast(I32),
            )
        cand_sb = load_list(cand, "cand_sb")
        w1_raw = new([P, PACK, H], F32, "w1_raw")
        nc.sync.dma_start(w1_raw[:], w1.rearrange("(p j) c -> p j c", j=PACK))
        table_words = new([P, T], I32, "table_words")
        nc.sync.dma_start(table_words[:], x_words[0].rearrange("p n r -> p (n r)").bitcast(I32))
        wb_raw = new([P, PACK, V], F32, "wb_raw")
        nc.sync.dma_start(wb_raw[:], wb.rearrange("(p j) v -> p j v", j=PACK))
        n1_sb = load_list(n1, "n1_sb")
        n3_sb = load_list(n3, "n3_sb")
        n2_sb = load_list(n2, "n2_sb")
        gs_sb = new([P, PACK], F32, "gs_sb")
        nc.gpsimd.dma_start(gs_sb[:], gs.rearrange("(p t) o -> p (t o)", t=PACK))

        warm_in = new([P, 1], F32, "warm_in")
        nc.vector.memset(warm_in[:], 1.0)
        warm_out = new([P, 1], F32, "warm_out")
        nc.scalar.activation(warm_out[:], warm_in[:], ACT.Sqrt)

        def padded_window(engine, width, name):
            tile = new([P, 2 * width], F32, name)
            engine.memset(tile[:, width:], 0.0)
            return tile

        y_sq = [padded_window(nc.vector, S, f"y_sq{t}") for t in range(PACK - 1)]
        y_sq.append(new([P, S], F32, f"y_sq{PACK - 1}"))
        b_sb = [padded_window(nc.gpsimd, V, f"b_sb{t}") for t in range(PACK)]
        a_sb = [padded_window(nc.gpsimd, V, f"a_sb{t}") for t in range(PACK)]

        def gather_scales(list_sb, name):
            picked = new([P, S], U8, name)
            nc.vector.tensor_copy(picked[:], table_scales[:].indirect(list_sb[:]))
            return picked

        def deal_scales(picked, name, tag=None):
            dealt = new([P, C], U8, name, tag)
            nc.vector.tensor_copy(
                dealt[:].rearrange("p (t m) -> p t m", t=PACK),
                picked[:].rearrange("p (m t) -> p t m", t=PACK),
            )
            return dealt

        xq_scales = gather_scales(offs_sb, "xq_scales")
        cb_picked = gather_scales(cb_sb, "cb_picked")
        cand_picked = gather_scales(cand_sb, "cand_picked")
        cb_scales = deal_scales(cb_picked, "cb_scales")

        def cast_w1(u):
            pair = new([P, 2, P, PACK], BF16, f"w1_bf{u}")
            nc.scalar.copy(
                pair[:].rearrange("p t m j -> p m j t"),
                w1_raw[:].rearrange("p j (m t) -> p m j t", t=PACK)[:, :, :, 2 * u : 2 * u + 2],
            )
            return pair

        def quantize_w1(pair, u):
            codes = new([P, 2 * P], U32, f"w1_codes{u}", tag="w1_codes")
            scales = new([P, 2 * P], U8, f"w1_scales{u}", tag="w1_scales")
            nc.vector.quantize_mx(
                out=codes[:].bitcast(FP8X4),
                scales=scales[:],
                in_=pair[:].rearrange("p t m j -> p (t m j)"),
            )
            return codes, scales

        words = table_words[:].bitcast(U32)
        w1_bf = [cast_w1(u) for u in range(2)]
        codes, scales = quantize_w1(w1_bf[0], 0)
        xq_words = []
        for h in range(2):
            picked = new([P, HALF_S], U32, f"xq_words{h}")
            nc.vector.tensor_copy(picked[:], words.indirect(offs_sb[:, 16 * h : 16 * (h + 1)]))
            xq_words.append(picked)

        def project(dest, codes, scales, e, h):
            rows = slice(e * P, (e + 1) * P)
            nc.tensor.matmul_mx(
                out=dest,
                lhsT=codes[:, rows].bitcast(FP8X4),
                lhsT_scale=scales[:, rows],
                rhs=xq_words[h][:].bitcast(FP8X4),
                rhs_scale=xq_scales[:, h * HALF_S : (h + 1) * HALF_S],
                start=True,
                stop=True,
            )

        for h in range(2):
            for t in range(2):
                half = psum.tile([P, HALF_S], F32, name=f"y_half{t}{h}", tag=f"bank{4 * (1 - h) + t}")
                project(half[:], codes, scales, t, h)
                nc.scalar.activation(y_sq[t][:, h * HALF_S : (h + 1) * HALF_S], half[:], ACT.Square)
        codes, scales = quantize_w1(w1_bf[1], 1)
        y_ps = {t: psum.tile([P, S], F32, name=f"y_ps{t}", tag=f"bank{t}") for t in (2, 3)}
        for t in (2, 3):
            for h in range(2):
                project(y_ps[t][:, h * HALF_S : (h + 1) * HALF_S], codes, scales, t - 2, h)

        def gather_words_dealt(list_sb, name, tag=None):
            dealt = new([P, C], U32, name, tag)
            nc.vector.tensor_copy(
                dealt[:].rearrange("p (t m) -> p m t", t=PACK), words.indirect(list_sb[:])
            )
            return dealt

        y_last = new([P, S], F32, "y_last")

        cb_words = gather_words_dealt(cb_sb, "cb_words")
        wb_bf = new([P, V, PACK], BF16, "wb_bf")
        nc.vector.tensor_copy(
            wb_bf[:].rearrange("p (c i) j -> p c j i", i=4),
            wb_raw[:].rearrange("p j (c i) -> p c j i", i=4),
        )
        cand_words = gather_words_dealt(cand_sb, "cand_words", tag="w1_bf1")
        wb_codes = new([P, V], U32, "wb_codes")
        wb_scales = new([P, V], U8, "wb_scales")
        nc.vector.quantize_mx(
            out=wb_codes[:].bitcast(FP8X4),
            scales=wb_scales[:],
            in_=wb_bf[:].rearrange("p v j -> p (v j)"),
        )
        nc.vector.tensor_copy(y_last[:], y_ps[PACK - 1][:])
        nc.vector.tensor_tensor(y_sq[PACK - 1][:], y_last[:], y_last[:], ALU.mult)

        b_banks = [psum.tile([P, 2, V], F32, name=f"b_bank{u}", tag=f"bank{6 + u}") for u in range(2)]
        b_ps = [b_banks[t // 2][:, t % 2, :] for t in range(PACK)]
        for t in range(PACK):
            rows = slice(t * P, (t + 1) * P)
            nc.tensor.matmul_mx(
                out=b_ps[t],
                lhsT=cb_words[:, rows].bitcast(FP8X4),
                lhsT_scale=cb_scales[:, rows],
                rhs=wb_codes[:].bitcast(FP8X4),
                rhs_scale=wb_scales[:],
                start=True,
                stop=True,
            )

        cand_scales = deal_scales(cand_picked, "cand_scales", tag="xq_scales")

        lined = new([P, PACK, S], F32, "lined")
        ms = new([P, PACK, V], F32, "ms")
        halves = (slice(0, HALF_V), slice(HALF_V, V))

        def add_pairs(dest, entries):
            pairs = entries.rearrange("p (v e) -> p v e", e=2)
            nc.vector.scalar_tensor_tensor(dest, pairs[:, :, 0], EPS, pairs[:, :, 1], ALU.add, ALU.add)

        nc.scalar.activation(y_sq[2][:, :S], y_ps[2][:], ACT.Square)
        last = PACK - 1
        for t in range(last):
            nc.scalar.activation(lined[:, t, :], y_sq[t][:].indirect(n1_sb[:]), ACT.Copy)
        for h in range(2):
            nc.scalar.activation(
                lined[:, last, h * HALF_S : (h + 1) * HALF_S],
                y_sq[last][:].indirect(n1_sb[:, 16 * h : 16 * (h + 1)]),
                ACT.Copy,
            )
        for t in range(2):
            nc.vector.tensor_copy(b_sb[t][:, :V], b_ps[t])
        add_pairs(
            ms[:, :last, :].rearrange("p t v -> p (t v)"),
            lined[:, :last, :].rearrange("p t s -> p (t s)"),
        )
        for h in range(2):
            add_pairs(ms[:, last, halves[h]], lined[:, last, h * HALF_S : (h + 1) * HALF_S])
        for t in range(2, PACK):
            nc.vector.tensor_copy(b_sb[t][:, :V], b_ps[t])

        z_bf = []
        for h in range(2):
            root = new([P, PACK, HALF_V], F32, f"root{h}")
            nc.scalar.activation(root[:], ms[:, :, halves[h]], ACT.Sqrt)
            half = new([P, HALF_V, PACK], BF16, f"z_bf{h}")
            nc.vector.tensor_tensor(
                half[:].rearrange("p (c i) t -> p c t i", i=4),
                root[:].rearrange("p t (c i) -> p c t i", i=4),
                gs_sb[:].unsqueeze(1).unsqueeze(3).to_broadcast([P, HALF_V // 4, PACK, 4]),
                ALU.mult,
            )
            z_bf.append(half)

        a_lo = [psum.tile([P, 2, HALF_V], F32, name=f"a_lo{u}", tag=f"bank{u}") for u in range(2)]
        a_hi = [psum.tile([P, HALF_V], F32, name=f"a_hi{t}", tag=f"bank{2 + t}") for t in range(PACK)]
        a_ps = [[a_lo[t // 2][:, t % 2, :] for t in range(PACK)], [a_hi[t][:] for t in range(PACK)]]
        for h in range(2):
            z_codes = new([P, HALF_V], U32, f"z_codes{h}")
            z_scales = new([P, HALF_V], U8, f"z_scales{h}")
            nc.vector.quantize_mx(
                out=z_codes[:].bitcast(FP8X4),
                scales=z_scales[:],
                in_=z_bf[h][:].rearrange("p v t -> p (v t)"),
            )
            for t in range(PACK):
                rows = slice(t * P, (t + 1) * P)
                nc.tensor.matmul_mx(
                    out=a_ps[h][t],
                    lhsT=cand_words[:, rows].bitcast(FP8X4),
                    lhsT_scale=cand_scales[:, rows],
                    rhs=z_codes[:].bitcast(FP8X4),
                    rhs_scale=z_scales[:],
                    start=True,
                    stop=True,
                )

        def look_up_pairs(found, window, list_sb):
            nc.scalar.activation(found, window[:].indirect(list_sb[:]), ACT.Copy)

        b_n3_all = new([P, PACK, V], F32, "b_n3_all", tag="lined")
        b_n3 = [b_n3_all[:, t, :] for t in range(PACK)]
        for t in range(PACK):
            look_up_pairs(b_n3[t], b_sb[t], n3_sb)

        for t in range(PACK):
            for h in range(2):
                nc.vector.tensor_scalar(a_sb[t][:, halves[h]], a_ps[h][t], OUT_SCALE, None, ALU.mult)
        first = [new([P, V], F32, f"first{t}") for t in range(PACK)]
        for t in range(PACK):
            if t < 2:
                for h in range(2):
                    nc.vector.scalar_tensor_tensor(
                        first[t][:, halves[h]],
                        a_ps[h][t],
                        OUT_SCALE,
                        b_n3[t][:, halves[h]],
                        ALU.mult,
                        ALU.mult,
                    )
            else:
                nc.gpsimd.tensor_tensor(first[t][:], a_sb[t][:, :V], b_n3[t], ALU.mult)
        out_rows = out.rearrange("(p t) v -> p t v", t=PACK)
        for t in range(PACK):
            a_n2 = new([P, V], F32, f"a_n2_{t}")
            look_up_pairs(a_n2[:], a_sb[t], n2_sb)
            second = new([P, V], F32, f"second{t}")
            nc.vector.tensor_tensor(second[:], b_ps[t], a_n2[:], ALU.mult)
            result = new([P, V], F32, f"result{t}")
            nc.vector.tensor_tensor(result[:], first[t][:], second[:], ALU.subtract)
            nc.sync.dma_start(out_rows[:, t, :], result[:])
